import numpy as np
import ml_dtypes

BF16 = ml_dtypes.bfloat16


def bf(x):
    return np.asarray(x, np.float32).astype(BF16)


def f32(x):
    return np.asarray(x, np.float32)


def f64(x):
    return np.asarray(x).astype(np.float64)


def striped(idx):
    return np.tile(idx.reshape(-1, 16).T, (8, 1))


S, K, M, N, V, D = 256, 256, 128, 256, 16, 16


def setup_inputs():
    return {"table": bf(np.random.standard_normal((K, S))), "w": bf(np.random.standard_normal((K, M)) / np.sqrt(K)), "x": bf(np.random.standard_normal((K, V))), "wc": bf(np.random.standard_normal((K, M)) / np.sqrt(K)), "b": f32(0.5 * np.random.standard_normal((M, 1))), "offs": striped(np.random.permutation(np.tile(np.arange(S), 2))[:N])}


def reference(table, w, x, wc, b, offs):
    idx = offs[:16].T.reshape(-1)
    y = (f64(w).T @ f64(table)[:, idx]).reshape(M, V, D)
    u = f64(wc).T @ f64(x) + f64(b)
    z = y + u[:, :, None]
    z = np.maximum(z, 0.0)
    return z.max(axis=2)

@@ -1,0 +1,52 @@
+import concourse.mybir as mybir
+
+P = 128
+K, S, M, N, V = 256, 256, 128, 256, 16
+D = N // V
+KB = K // P
+
+FLOPS = 2 * K * M * (N + V)
+
+BF16, F32, U16 = mybir.dt.bfloat16, mybir.dt.float32, mybir.dt.uint16
+ADD, MAX = mybir.AluOpType.add, mybir.AluOpType.max
+
+
+def by_block(dram):
+    return dram.rearrange("(p a) c -> p a c", a=KB)
+
+
+def tile_rows_ecv_rep_relu_kernel(tc, table, w, x, wc, b, offs, out):
+    nc = tc.nc
+    with (
+        tc.tile_pool(name="sbuf", bufs=1) as sbuf,
+        tc.psum_pool(name="psum", bufs=1) as psum,
+    ):
+        offsets = sbuf.tile([P, N // 16], U16)
+        points = sbuf.tile([P, KB, S], BF16)
+        w_nbr = sbuf.tile([P, KB, M], BF16)
+        w_ctr = sbuf.tile([P, KB, M], BF16)
+        centres = sbuf.tile([P, KB, V], BF16)
+        bias = sbuf.tile([M, 1], F32)
+
+        nc.sync.dma_start(points[:], by_block(table))
+        nc.sync.dma_start(offsets[:], offs)
+        nc.scalar.dma_start(w_nbr[:], by_block(w))
+        nc.scalar.dma_start(w_ctr[:], by_block(wc))
+        nc.scalar.dma_start(centres[:], by_block(x))
+        nc.scalar.dma_start(bias[:], b)
+
+        y = psum.tile([M, N], F32)
+        for a in range(KB):
+            picked = points[:, a, :].indirect(offsets[:])
+            nc.tensor.matmul(y[:], w_nbr[:, a, :], picked, start=(a == 0), stop=(a == KB - 1))
+        u = psum.tile([M, V], F32)
+        for a in range(KB):
+            nc.tensor.matmul(u[:], w_ctr[:, a, :], centres[:, a, :], start=(a == 0), stop=(a == KB - 1))
+
+        largest = sbuf.tile([M, V], F32)
+        nc.vector.tensor_reduce(largest[:], y[:].rearrange("m (v t) -> m v t", t=D), mybir.AxisListType.X, MAX)
+        summed = sbuf.tile([M, V], F32)
+        nc.vector.scalar_tensor_tensor(summed[:], u[:], bias[:], largest[:], ADD, ADD)
+        result = sbuf.tile([M, V], F32)
+        nc.vector.tensor_scalar_max(result[:], summed[:], 0.0)
+        nc.sync.dma_start(out, result[:])

@@ -29,11 +29,11 @@ def tile_rows_ecv_rep_relu_kernel(tc, table, w, x, wc, b, offs, out):
         bias = sbuf.tile([M, 1], F32)
 
         nc.sync.dma_start(points[:], by_block(table))
-        nc.sync.dma_start(offsets[:], offs)
         nc.scalar.dma_start(w_nbr[:], by_block(w))
-        nc.scalar.dma_start(w_ctr[:], by_block(wc))
-        nc.scalar.dma_start(centres[:], by_block(x))
-        nc.scalar.dma_start(bias[:], b)
+        nc.sync.dma_start(offsets[:], offs)
+        nc.sync.dma_start(w_ctr[:], by_block(wc))
+        nc.sync.dma_start(centres[:], by_block(x))
+        nc.sync.dma_start(bias[:], b)
 
         y = psum.tile([M, N], F32)
         for a in range(KB):

@@ -4,6 +4,7 @@ P = 128
 K, S, M, N, V = 256, 256, 128, 256, 16
 D = N // V
 KB = K // P
+PIECES = 2
 
 FLOPS = 2 * K * M * (N + V)
 
@@ -35,16 +36,18 @@ def tile_rows_ecv_rep_relu_kernel(tc, table, w, x, wc, b, offs, out):
         nc.sync.dma_start(centres[:], by_block(x))
         nc.sync.dma_start(bias[:], b)
 
-        y = psum.tile([M, N], F32)
-        for a in range(KB):
-            picked = points[:, a, :].indirect(offsets[:])
-            nc.tensor.matmul(y[:], w_nbr[:, a, :], picked, start=(a == 0), stop=(a == KB - 1))
+        largest = sbuf.tile([M, V], F32)
+        for h in range(PIECES):
+            group = slice(h * V // PIECES, (h + 1) * V // PIECES)
+            y = psum.tile([M, N // PIECES], F32, name=f"y{h}")
+            for a in range(KB):
+                picked = points[:, a, :].indirect(offsets[:, group])
+                nc.tensor.matmul(y[:], w_nbr[:, a, :], picked, start=(a == 0), stop=(a == KB - 1))
+            nc.vector.tensor_reduce(largest[:, group], y[:].rearrange("m (v t) -> m v t", t=D), mybir.AxisListType.X, MAX)
         u = psum.tile([M, V], F32)
         for a in range(KB):
             nc.tensor.matmul(u[:], w_ctr[:, a, :], centres[:, a, :], start=(a == 0), stop=(a == KB - 1))
 
-        largest = sbuf.tile([M, V], F32)
-        nc.vector.tensor_reduce(largest[:], y[:].rearrange("m (v t) -> m v t", t=D), mybir.AxisListType.X, MAX)
         summed = sbuf.tile([M, V], F32)
         nc.vector.scalar_tensor_tensor(summed[:], u[:], bias[:], largest[:], ADD, ADD)
         result = sbuf.tile([M, V], F32)

import concourse.mybir as mybir

P = 128
K, S, M, N, V = 256, 256, 128, 256, 16
D = N // V
KB = K // P
PIECES = 2

FLOPS = 2 * K * M * (N + V)

BF16, F32, U16 = mybir.dt.bfloat16, mybir.dt.float32, mybir.dt.uint16
ADD, MAX = mybir.AluOpType.add, mybir.AluOpType.max


def by_block(dram):
    return dram.rearrange("(p a) c -> p a c", a=KB)


def tile_rows_ecv_rep_relu_kernel(tc, table, w, x, wc, b, offs, out):
    nc = tc.nc
    with (
        tc.tile_pool(name="sbuf", bufs=1) as sbuf,
        tc.psum_pool(name="psum", bufs=1) as psum,
    ):
        offsets = sbuf.tile([P, N // 16], U16)
        points = sbuf.tile([P, KB, S], BF16)
        w_nbr = sbuf.tile([P, KB, M], BF16)
        w_ctr = sbuf.tile([P, KB, M], BF16)
        centres = sbuf.tile([P, KB, V], BF16)
        bias = sbuf.tile([M, 1], F32)

        nc.sync.dma_start(points[:], by_block(table))
        nc.scalar.dma_start(w_nbr[:], by_block(w))
        nc.sync.dma_start(offsets[:], offs)
        nc.sync.dma_start(w_ctr[:], by_block(wc))
        nc.sync.dma_start(centres[:], by_block(x))
        nc.sync.dma_start(bias[:], b)

        largest = sbuf.tile([M, V], F32)
        for h in range(PIECES):
            group = slice(h * V // PIECES, (h + 1) * V // PIECES)
            y = psum.tile([M, N // PIECES], F32, name=f"y{h}")
            for a in range(KB):
                picked = points[:, a, :].indirect(offsets[:, group])
                nc.tensor.matmul(y[:], w_nbr[:, a, :], picked, start=(a == 0), stop=(a == KB - 1))
            nc.vector.tensor_reduce(largest[:, group], y[:].rearrange("m (v t) -> m v t", t=D), mybir.AxisListType.X, MAX)
        u = psum.tile([M, V], F32)
        for a in range(KB):
            nc.tensor.matmul(u[:], w_ctr[:, a, :], centres[:, a, :], start=(a == 0), stop=(a == KB - 1))

        summed = sbuf.tile([M, V], F32)
        nc.vector.scalar_tensor_tensor(summed[:], u[:], bias[:], largest[:], ADD, ADD)
        result = sbuf.tile([M, V], F32)
        nc.vector.tensor_scalar_max(result[:], summed[:], 0.0)
        nc.sync.dma_start(out, result[:])
